import numpy as np
import ml_dtypes


def mxq(x, axis, fmt="e4m3"):
    dtype, down = {"e4m3": (ml_dtypes.float8_e4m3fn, 7), "e5m2": (ml_dtypes.float8_e5m2, 14)}[fmt]
    v = np.moveaxis(np.asarray(x, np.float32).astype(ml_dtypes.bfloat16).astype(np.float64), axis, -1)
    blocks = v.reshape(v.shape[:-1] + (-1, 32))
    amax = np.abs(blocks).max(-1, keepdims=True)
    byte = np.maximum(np.where(amax > 0, np.frexp(amax)[1] - 1 + 127, 0) - down, 1)
    scale = np.exp2(byte - 127.0)
    codes = (blocks / scale).astype(np.float32).astype(dtype).astype(np.float64)
    return np.moveaxis((codes * scale).reshape(v.shape), -1, axis)


WIDE = False


def mx_kscale(k):
    if not WIDE:
        return np.ones(k)
    levels = np.array([10, -10, 5, -5, 0])
    if k % 512:
        return np.exp2(np.random.permutation(np.resize(levels, k // 32))).repeat(32)
    a = np.empty((k // 512, 16))
    for p in range(k // 512):
        a[p, :8] = np.random.permutation(np.resize(levels, 8))
        for g in range(8):
            far = levels[np.abs(levels - a[p, g]) >= 10]
            a[p, g + 8] = far[np.random.randint(len(far))]
    return np.exp2(a.ravel()).repeat(32)


def f64(x):
    return np.asarray(x).astype(np.float64)


def striped(idx):
    return np.tile(idx.reshape(-1, 16).T, (8, 1)).astype(np.uint16)


def unstriped(offs):
    return offs[:16].T.reshape(-1).astype(np.int64)


def pack_weight(w):
    k, n = w.shape
    w = f64(np.asarray(w, np.float32).astype(ml_dtypes.bfloat16)).reshape(k // 32, 32, n)
    amax = np.abs(w).max(1)
    byte = np.clip(np.where(amax > 0, np.frexp(amax)[1] - 1 + 127 - 7, 1), 1, 254)
    scaled = (w * np.exp2(127.0 - byte)[:, None, :]).reshape(k, n).astype(np.float32)
    words = np.ascontiguousarray(scaled.reshape(k // 512, 128, 4, n).transpose(0, 1, 3, 2)).astype(ml_dtypes.float8_e4m3fn).view(np.uint8)
    return words, np.ascontiguousarray(byte.astype(np.uint8).reshape(k // 512, 16, n))


def unpack_weight(words, scales):
    g, p, n, _ = words.shape
    vals = np.ascontiguousarray(words).view(ml_dtypes.float8_e4m3fn).astype(np.float64) * np.repeat(np.exp2(scales.astype(np.float64) - 127.0), 8, axis=1)[..., None]
    return vals.transpose(0, 1, 3, 2).reshape(g * 512, n)


def gelu(v):
    return 0.5 * v * (1.0 + np.tanh(np.sqrt(2.0 / np.pi) * (v + 0.044715 * v**3)))

def planes(y):
    n, m = y.shape
    v = y.astype(np.float32).astype(ml_dtypes.bfloat16).astype(np.float64).reshape(n // 32, 32, m)
    top = np.abs(v).max(1)
    byte = np.clip(np.where(top > 0, np.frexp(top)[1] - 1 + 127 - 7, 1), 1, 254)
    codes = (v * np.exp2(127.0 - byte)[:, None, :]).reshape(n, m).astype(np.float32).astype(ml_dtypes.float8_e4m3fn).view(np.uint8)
    words = codes.reshape(n // 512, 128, 4, m).transpose(0, 1, 3, 2)
    return np.ascontiguousarray(words), np.ascontiguousarray(byte.astype(np.uint8).reshape(n // 512, 16, m))


K, T, S, V, H = 512, 2048, 512, 512, 512


def setup_inputs():
    n = np.random.standard_normal
    s = mx_kscale(K)[:, None]
    packed_xT = pack_weight(n((K, T)) * s)
    packed_w1 = pack_weight(n((K, H)) / np.sqrt(K) / s)
    return {
        "x_words": packed_xT[0],
        "x_scales": packed_xT[1],
        "w1_words": packed_w1[0],
        "w1_scales": packed_w1[1],
        "gs": (np.random.uniform(0.5, 1.5, (K, 1)) / s).astype(np.float32),
        "offs": striped(np.random.permutation(T)[:S]),
        "cand": striped(np.random.permutation(T)[:V]),
    }


def reference(x_words, x_scales, w1_words, w1_scales, gs, offs, cand):
    x_cand = unpack_weight(x_words, x_scales)[:, unstriped(cand)]
    xq = unpack_weight(x_words, x_scales)[:, unstriped(offs)]
    h = gelu(unpack_weight(w1_words, w1_scales).T @ xq)
    z = f64(gs) * h
    s = 0.0625 * ((x_cand.T @ mxq(z, 0, "e4m3")))
    out_0 = 4.0 * np.tanh(0.25 * s)
    return (out_0,) + planes(out_0)

@@ -1,0 +1,164 @@
+from contextlib import ExitStack
+
+import concourse.mybir as mybir
+
+K, T, S, V, H = 512, 2048, 512, 512, 512
+FLOPS = 2 * K * H * S + 2 * K * V * S
+
+F32 = mybir.dt.float32
+BF16 = mybir.dt.bfloat16
+I32 = mybir.dt.int32
+U32 = mybir.dt.uint32
+U16 = mybir.dt.uint16
+U8 = mybir.dt.uint8
+FP8X4 = mybir.dt.float8_e4m3fn_x4
+ACT = mybir.ActivationFunctionType
+MULT = mybir.AluOpType.mult
+
+P = 128
+PACK = 4
+QUADS = 4
+CHUNK = 128
+CHUNKS = S // CHUNK
+HALF = S // 2
+W_ROW = 4
+SCALAR_CAP = (0, 2, 3)
+
+
+def tile_picked_candcap_gelu_po_kernel(
+    tc, x_words, x_scales, w1_words, w1_scales, gs, offs, cand, out_0, out_1, out_2
+):
+    nc = tc.nc
+    with ExitStack() as ctx:
+        sb = ctx.enter_context(tc.tile_pool(name="sb", bufs=1))
+        ps = ctx.enter_context(tc.psum_pool(name="ps", bufs=1))
+
+        def tile(name, shape, dtype, tag=""):
+            return sb.tile(shape, dtype, name=name, tag=tag or name, align_bytes=64)
+
+        offs_t = tile("offs_t", [P, S // 16], U16)
+        cand_t = tile("cand_t", [P, V // 16], U16)
+        xw = tile("xw", [P, T], I32)
+        xs = tile("xs", [P, T], U8)
+        ww = tile("ww", [P, H], I32)
+        ws = tile("ws", [P, H], U8, tag="undealt")
+        gs_t = tile("gs_t", [P, PACK], F32)
+
+        nc.vector.memset(xs[:].bitcast(I32), 0)
+        nc.vector.memset(ws[:].bitcast(I32), 0)
+        nc.sync.dma_start(offs_t[:], offs)
+        nc.sync.dma_start(cand_t[:], cand)
+        nc.sync.dma_start(ww[:], w1_words[0].rearrange("p n t -> p (n t)").bitcast(I32))
+        for q in range(QUADS):
+            nc.scalar.dma_start(xs[32 * q : 32 * q + 4, :].bitcast(I32), x_scales[0, 4 * q : 4 * q + 4, :].bitcast(I32))
+        nc.sync.dma_start(xw[:], x_words[0].rearrange("p n t -> p (n t)").bitcast(I32))
+        for q in range(QUADS):
+            eng = nc.gpsimd if q < 2 else nc.scalar
+            r = 32 * q + W_ROW
+            eng.dma_start(ws[r : r + 4, :].bitcast(I32), w1_scales[0, 4 * q : 4 * q + 4, :].bitcast(I32))
+        nc.gpsimd.dma_start(gs_t[:], gs.rearrange("(p t) o -> p (t o)", t=PACK))
+
+        def deal(dst, src):
+            nc.vector.tensor_copy(
+                dst.rearrange("p (t m) -> p t m", t=PACK), src.rearrange("p (m t) -> p t m", t=PACK)
+            )
+
+        wwd = tile("wwd", [P, H], U32)
+        wsd = tile("wsd", [P, H], U8)
+        deal(wwd[:], ww[:].bitcast(U32))
+
+        tok_s = tile("tok_s", [P, S], U8)
+        can_s = tile("can_s", [P, V], U8)
+        can_sd = tile("can_sd", [P, V], U8)
+        nc.vector.tensor_copy(tok_s[:], xs[:].indirect(offs_t[:]))
+        deal(wsd[:], ws[:])
+        nc.vector.tensor_copy(can_s[:], xs[:].indirect(cand_t[:]))
+        deal(can_sd[:], can_s[:])
+
+        tok_w = tile("tok_w", [P, S], U32)
+        for a in range(2):
+            nc.vector.tensor_copy(
+                tok_w[:, a * HALF : (a + 1) * HALF],
+                xw[:].bitcast(U32).indirect(offs_t[:, a * HALF // 16 : (a + 1) * HALF // 16]),
+            )
+        can_w = tile("can_w", [P, V], U32, tag="undealt")
+        can_wd = tile("can_wd", [P, V], U32)
+        nc.vector.tensor_copy(can_w[:], xw[:].bitcast(U32).indirect(cand_t[:]))
+        deal(can_wd[:], can_w[:])
+
+        cols = [slice(c * CHUNK, (c + 1) * CHUNK) for c in range(CHUNKS)]
+        hid = []
+        for c in range(CHUNKS):
+            bank = ps.tile([P, PACK, CHUNK], F32, name=f"pre{c}")
+            for t in range(PACK):
+                nc.tensor.matmul_mx(
+                    out=bank[:, t, :],
+                    lhsT=wwd[:, t * P : (t + 1) * P].bitcast(FP8X4),
+                    lhsT_scale=wsd[W_ROW:P, t * P : (t + 1) * P],
+                    rhs=tok_w[:, cols[c]].bitcast(FP8X4),
+                    rhs_scale=tok_s[:, cols[c]],
+                    start=True,
+                    stop=True,
+                )
+            h = tile(f"h{c}", [P, CHUNK, PACK], F32)
+            nc.scalar.activation(h[:], bank[:].rearrange("p t n -> p n t"), ACT.Gelu_apprx_tanh)
+            hid.append(h)
+
+        z_w = tile("z_w", [P, S], U32)
+        z_s = tile("z_s", [P, S], U8)
+        gain = gs_t[:].unsqueeze(1).to_broadcast([P, CHUNK, PACK])
+        zb = [tile(f"zb{c}", [P, CHUNK, PACK], BF16) for c in range(CHUNKS)]
+
+        def scale_z(c):
+            nc.vector.tensor_tensor(zb[c][:], hid[c][:], gain, MULT)
+
+        def quant_z(c):
+            nc.vector.quantize_mx(
+                out=z_w[:, cols[c]].bitcast(FP8X4), scales=z_s[:, cols[c]], in_=zb[c][:].rearrange("p n t -> p (n t)")
+            )
+
+        scale_z(0)
+        for c in range(1, CHUNKS):
+            scale_z(c)
+            quant_z(c - 1)
+        quant_z(CHUNKS - 1)
+
+        th = []
+        for c in range(CHUNKS):
+            bank = ps.tile([P, PACK, CHUNK], F32, name=f"score{c}")
+            for t in range(PACK):
+                nc.tensor.matmul_mx(
+                    out=bank[:, t, :],
+                    lhsT=can_wd[:, t * P : (t + 1) * P].bitcast(FP8X4),
+                    lhsT_scale=can_sd[:, t * P : (t + 1) * P],
+                    rhs=z_w[:, cols[c]].bitcast(FP8X4),
+                    rhs_scale=z_s[:, cols[c]],
+                    start=True,
+                    stop=True,
+                )
+            tt = tile(f"th{c}", [P, PACK, CHUNK], F32)
+            nc.scalar.activation(tt[:], bank[:], ACT.Tanh, scale=0.25 * 0.0625)
+            th.append(tt)
+
+        o_w = tile("o_w", [P, S], U32)
+        o_s = tile("o_s", [P, S], U8)
+        out_rows = out_0.rearrange("(p t) n -> p t n", t=PACK)
+        words_out = out_1[0].rearrange("p n t -> p (n t)").bitcast(I32)
+        for c in range(CHUNKS):
+            y = tile(f"y{c}", [P, PACK, CHUNK], F32)
+            if c in SCALAR_CAP:
+                nc.scalar.mul(y[:], th[c][:], 4.0)
+            else:
+                nc.vector.tensor_scalar_mul(y[:], th[c][:], 4.0)
+            nc.sync.dma_start(out_rows[:, :, cols[c]], y[:])
+            yb = tile(f"yb{c}", [P, CHUNK, PACK], BF16)
+            nc.vector.tensor_scalar_mul(yb[:], th[c][:].rearrange("p t n -> p n t"), 4.0)
+            nc.vector.quantize_mx(
+                out=o_w[:, cols[c]].bitcast(FP8X4), scales=o_s[:, cols[c]], in_=yb[:].rearrange("p n t -> p (n t)")
+            )
+            if c % 2 == 1:
+                half = slice((c - 1) * CHUNK, (c + 1) * CHUNK)
+                nc.sync.dma_start(words_out[:, half], o_w[:, half].bitcast(I32))
+        for q in range(QUADS):
+            eng = nc.sync if q % 2 == 0 else nc.scalar
+            eng.dma_start(out_2[0, 4 * q : 4 * q + 4, :].bitcast(I32), o_s[32 * q : 32 * q + 4, :].bitcast(I32))

@@ -22,7 +22,7 @@ CHUNK = 128
 CHUNKS = S // CHUNK
 HALF = S // 2
 W_ROW = 4
-SCALAR_CAP = (0, 2, 3)
+SCALAR_CAP = (0, 1, 2, 3)
 
 
 def tile_picked_candcap_gelu_po_kernel(
@@ -38,34 +38,42 @@ def tile_picked_candcap_gelu_po_kernel(
 
         offs_t = tile("offs_t", [P, S // 16], U16)
         cand_t = tile("cand_t", [P, V // 16], U16)
-        xw = tile("xw", [P, T], I32)
+        zeros = tile("zeros", [P, H // PACK], I32, tag="table")
         xs = tile("xs", [P, T], U8)
         ww = tile("ww", [P, H], I32)
         ws = tile("ws", [P, H], U8, tag="undealt")
         gs_t = tile("gs_t", [P, PACK], F32)
 
         nc.vector.memset(xs[:].bitcast(I32), 0)
-        nc.vector.memset(ws[:].bitcast(I32), 0)
+        nc.vector.memset(zeros[:], 0)
+        nc.vector.tensor_copy(ws[:].bitcast(I32), zeros[:])
+        xw = tile("xw", [P, T], I32, tag="table")
         nc.sync.dma_start(offs_t[:], offs)
         nc.sync.dma_start(cand_t[:], cand)
         nc.sync.dma_start(ww[:], w1_words[0].rearrange("p n t -> p (n t)").bitcast(I32))
         for q in range(QUADS):
-            nc.scalar.dma_start(xs[32 * q : 32 * q + 4, :].bitcast(I32), x_scales[0, 4 * q : 4 * q + 4, :].bitcast(I32))
+            eng = nc.sync if q % 2 == 0 else nc.scalar
+            eng.dma_start(xs[32 * q : 32 * q + 4, :].bitcast(I32), x_scales[0, 4 * q : 4 * q + 4, :].bitcast(I32))
         nc.sync.dma_start(xw[:], x_words[0].rearrange("p n t -> p (n t)").bitcast(I32))
         for q in range(QUADS):
-            eng = nc.gpsimd if q < 2 else nc.scalar
+            eng = nc.sync
             r = 32 * q + W_ROW
             eng.dma_start(ws[r : r + 4, :].bitcast(I32), w1_scales[0, 4 * q : 4 * q + 4, :].bitcast(I32))
-        nc.gpsimd.dma_start(gs_t[:], gs.rearrange("(p t) o -> p (t o)", t=PACK))
+        nc.sync.dma_start(gs_t[:], gs.rearrange("(p t) o -> p (t o)", t=PACK))
 
         def deal(dst, src):
             nc.vector.tensor_copy(
                 dst.rearrange("p (t m) -> p t m", t=PACK), src.rearrange("p (m t) -> p t m", t=PACK)
             )
 
+        def deal_words(dst, src):
+            nc.vector.tensor_copy(
+                dst.rearrange("p (t b i) -> p b t i", t=PACK, i=4), src.rearrange("p (b i t) -> p b t i", t=PACK, i=4)
+            )
+
         wwd = tile("wwd", [P, H], U32)
         wsd = tile("wsd", [P, H], U8)
-        deal(wwd[:], ww[:].bitcast(U32))
+        deal_words(wwd[:], ww[:].bitcast(U32))
 
         tok_s = tile("tok_s", [P, S], U8)
         can_s = tile("can_s", [P, V], U8)
@@ -75,16 +83,18 @@ def tile_picked_candcap_gelu_po_kernel(
         nc.vector.tensor_copy(can_s[:], xs[:].indirect(cand_t[:]))
         deal(can_sd[:], can_s[:])
 
-        tok_w = tile("tok_w", [P, S], U32)
+        early_w = tile("early_w", [P, HALF], U32)
+        late_w = tile("late_w", [P, HALF + V], U32, tag="undealt")
+        tok_w = [early_w[:], late_w[:, :HALF]]
         for a in range(2):
             nc.vector.tensor_copy(
-                tok_w[:, a * HALF : (a + 1) * HALF],
+                tok_w[a],
                 xw[:].bitcast(U32).indirect(offs_t[:, a * HALF // 16 : (a + 1) * HALF // 16]),
             )
-        can_w = tile("can_w", [P, V], U32, tag="undealt")
+        can_w = late_w[:, HALF:]
         can_wd = tile("can_wd", [P, V], U32)
-        nc.vector.tensor_copy(can_w[:], xw[:].bitcast(U32).indirect(cand_t[:]))
-        deal(can_wd[:], can_w[:])
+        nc.vector.tensor_copy(can_w, xw[:].bitcast(U32).indirect(cand_t[:]))
+        deal_words(can_wd[:], can_w)
 
         cols = [slice(c * CHUNK, (c + 1) * CHUNK) for c in range(CHUNKS)]
         hid = []
@@ -95,7 +105,7 @@ def tile_picked_candcap_gelu_po_kernel(
                     out=bank[:, t, :],
                     lhsT=wwd[:, t * P : (t + 1) * P].bitcast(FP8X4),
                     lhsT_scale=wsd[W_ROW:P, t * P : (t + 1) * P],
-                    rhs=tok_w[:, cols[c]].bitcast(FP8X4),
+                    rhs=tok_w[c // 2][:, cols[c % 2]].bitcast(FP8X4),
                     rhs_scale=tok_s[:, cols[c]],
                     start=True,
                     stop=True,
@@ -152,7 +162,9 @@ def tile_picked_candcap_gelu_po_kernel(
                 nc.vector.tensor_scalar_mul(y[:], th[c][:], 4.0)
             nc.sync.dma_start(out_rows[:, :, cols[c]], y[:])
             yb = tile(f"yb{c}", [P, CHUNK, PACK], BF16)
-            nc.vector.tensor_scalar_mul(yb[:], th[c][:].rearrange("p t n -> p n t"), 4.0)
+            nc.vector.tensor_scalar_mul(
+                yb[:].rearrange("p (b i) t -> p b t i", i=4), th[c][:].rearrange("p t (b i) -> p b t i", i=4), 4.0
+            )
             nc.vector.quantize_mx(
                 out=o_w[:, cols[c]].bitcast(FP8X4), scales=o_s[:, cols[c]], in_=yb[:].rearrange("p n t -> p (n t)")
             )

@@ -22,7 +22,7 @@ CHUNK = 128
 CHUNKS = S // CHUNK
 HALF = S // 2
 W_ROW = 4
-SCALAR_CAP = (0, 1, 2, 3)
+SCALAR_CAP = (0, 3)
 
 
 def tile_picked_candcap_gelu_po_kernel(
@@ -45,7 +45,7 @@ def tile_picked_candcap_gelu_po_kernel(
         gs_t = tile("gs_t", [P, PACK], F32)
 
         nc.vector.memset(xs[:].bitcast(I32), 0)
-        nc.vector.memset(zeros[:], 0)
+        nc.gpsimd.memset(zeros[:], 0)
         nc.vector.tensor_copy(ws[:].bitcast(I32), zeros[:])
         xw = tile("xw", [P, T], I32, tag="table")
         nc.sync.dma_start(offs_t[:], offs)
@@ -61,8 +61,8 @@ def tile_picked_candcap_gelu_po_kernel(
             eng.dma_start(ws[r : r + 4, :].bitcast(I32), w1_scales[0, 4 * q : 4 * q + 4, :].bitcast(I32))
         nc.sync.dma_start(gs_t[:], gs.rearrange("(p t) o -> p (t o)", t=PACK))
 
-        def deal(dst, src):
-            nc.vector.tensor_copy(
+        def deal(eng, dst, src):
+            eng.tensor_copy(
                 dst.rearrange("p (t m) -> p t m", t=PACK), src.rearrange("p (m t) -> p t m", t=PACK)
             )
 
@@ -77,11 +77,9 @@ def tile_picked_candcap_gelu_po_kernel(
 
         tok_s = tile("tok_s", [P, S], U8)
         can_s = tile("can_s", [P, V], U8)
-        can_sd = tile("can_sd", [P, V], U8)
         nc.vector.tensor_copy(tok_s[:], xs[:].indirect(offs_t[:]))
-        deal(wsd[:], ws[:])
+        deal(nc.vector, wsd[:], ws[:])
         nc.vector.tensor_copy(can_s[:], xs[:].indirect(cand_t[:]))
-        deal(can_sd[:], can_s[:])
 
         early_w = tile("early_w", [P, HALF], U32)
         late_w = tile("late_w", [P, HALF + V], U32, tag="undealt")
@@ -91,10 +89,8 @@ def tile_picked_candcap_gelu_po_kernel(
                 tok_w[a],
                 xw[:].bitcast(U32).indirect(offs_t[:, a * HALF // 16 : (a + 1) * HALF // 16]),
             )
-        can_w = late_w[:, HALF:]
-        can_wd = tile("can_wd", [P, V], U32)
-        nc.vector.tensor_copy(can_w, xw[:].bitcast(U32).indirect(cand_t[:]))
-        deal_words(can_wd[:], can_w)
+        can_wd = late_w[:, HALF:]
+        nc.vector.tensor_copy(can_wd.rearrange("p (t m) -> p m t", t=PACK), xw[:].bitcast(U32).indirect(cand_t[:]))
 
         cols = [slice(c * CHUNK, (c + 1) * CHUNK) for c in range(CHUNKS)]
         hid = []
@@ -128,12 +124,23 @@ def tile_picked_candcap_gelu_po_kernel(
             )
 
         scale_z(0)
-        for c in range(1, CHUNKS):
+        can_sd = tile("can_sd", [P, V], U8, tag="h0")
+        deal(nc.vector, can_sd[:], can_s[:])
+        quant_z(0)
+        scale_z(1)
+        for c in range(2, CHUNKS):
             scale_z(c)
             quant_z(c - 1)
         quant_z(CHUNKS - 1)
 
         th = []
+        out_rows = out_0.rearrange("(p t) n -> p t n", t=PACK)
+
+        def cap(c, mul):
+            y = tile(f"y{c}", [P, PACK, CHUNK], F32)
+            mul(y[:], th[c][:], 4.0)
+            nc.sync.dma_start(out_rows[:, :, cols[c]], y[:])
+
         for c in range(CHUNKS):
             bank = ps.tile([P, PACK, CHUNK], F32, name=f"score{c}")
             for t in range(PACK):
@@ -149,22 +156,19 @@ def tile_picked_candcap_gelu_po_kernel(
             tt = tile(f"th{c}", [P, PACK, CHUNK], F32)
             nc.scalar.activation(tt[:], bank[:], ACT.Tanh, scale=0.25 * 0.0625)
             th.append(tt)
+            if c in SCALAR_CAP:
+                cap(c, nc.scalar.mul)
 
         o_w = tile("o_w", [P, S], U32)
         o_s = tile("o_s", [P, S], U8)
-        out_rows = out_0.rearrange("(p t) n -> p t n", t=PACK)
         words_out = out_1[0].rearrange("p n t -> p (n t)").bitcast(I32)
         for c in range(CHUNKS):
-            y = tile(f"y{c}", [P, PACK, CHUNK], F32)
-            if c in SCALAR_CAP:
-                nc.scalar.mul(y[:], th[c][:], 4.0)
-            else:
-                nc.vector.tensor_scalar_mul(y[:], th[c][:], 4.0)
-            nc.sync.dma_start(out_rows[:, :, cols[c]], y[:])
             yb = tile(f"yb{c}", [P, CHUNK, PACK], BF16)
             nc.vector.tensor_scalar_mul(
                 yb[:].rearrange("p (b i) t -> p b t i", i=4), th[c][:].rearrange("p t (b i) -> p b t i", i=4), 4.0
             )
+            if c not in SCALAR_CAP:
+                cap(c, nc.vector.tensor_scalar_mul)
             nc.vector.quantize_mx(
                 out=o_w[:, cols[c]].bitcast(FP8X4), scales=o_s[:, cols[c]], in_=yb[:].rearrange("p n t -> p (n t)")
             )
@@ -172,5 +176,5 @@ def tile_picked_candcap_gelu_po_kernel(
                 half = slice((c - 1) * CHUNK, (c + 1) * CHUNK)
                 nc.sync.dma_start(words_out[:, half], o_w[:, half].bitcast(I32))
         for q in range(QUADS):
-            eng = nc.sync if q % 2 == 0 else nc.scalar
+            eng = nc.sync if q == QUADS - 1 else nc.scalar
             eng.dma_start(out_2[0, 4 * q : 4 * q + 4, :].bitcast(I32), o_s[32 * q : 32 * q + 4, :].bitcast(I32))

from contextlib import ExitStack

import concourse.mybir as mybir

K, T, S, V, H = 512, 2048, 512, 512, 512
FLOPS = 2 * K * H * S + 2 * K * V * S

F32 = mybir.dt.float32
BF16 = mybir.dt.bfloat16
I32 = mybir.dt.int32
U32 = mybir.dt.uint32
U16 = mybir.dt.uint16
U8 = mybir.dt.uint8
FP8X4 = mybir.dt.float8_e4m3fn_x4
ACT = mybir.ActivationFunctionType
MULT = mybir.AluOpType.mult

P = 128
PACK = 4
QUADS = 4
CHUNK = 128
CHUNKS = S // CHUNK
HALF = S // 2
W_ROW = 4
SCALAR_CAP = (0, 3)


def tile_picked_candcap_gelu_po_kernel(
    tc, x_words, x_scales, w1_words, w1_scales, gs, offs, cand, out_0, out_1, out_2
):
    nc = tc.nc
    with ExitStack() as ctx:
        sb = ctx.enter_context(tc.tile_pool(name="sb", bufs=1))
        ps = ctx.enter_context(tc.psum_pool(name="ps", bufs=1))

        def tile(name, shape, dtype, tag=""):
            return sb.tile(shape, dtype, name=name, tag=tag or name, align_bytes=64)

        offs_t = tile("offs_t", [P, S // 16], U16)
        cand_t = tile("cand_t", [P, V // 16], U16)
        zeros = tile("zeros", [P, H // PACK], I32, tag="table")
        xs = tile("xs", [P, T], U8)
        ww = tile("ww", [P, H], I32)
        ws = tile("ws", [P, H], U8, tag="undealt")
        gs_t = tile("gs_t", [P, PACK], F32)

        nc.vector.memset(xs[:].bitcast(I32), 0)
        nc.gpsimd.memset(zeros[:], 0)
        nc.vector.tensor_copy(ws[:].bitcast(I32), zeros[:])
        xw = tile("xw", [P, T], I32, tag="table")
        nc.sync.dma_start(offs_t[:], offs)
        nc.sync.dma_start(cand_t[:], cand)
        nc.sync.dma_start(ww[:], w1_words[0].rearrange("p n t -> p (n t)").bitcast(I32))
        for q in range(QUADS):
            eng = nc.sync if q % 2 == 0 else nc.scalar
            eng.dma_start(xs[32 * q : 32 * q + 4, :].bitcast(I32), x_scales[0, 4 * q : 4 * q + 4, :].bitcast(I32))
        nc.sync.dma_start(xw[:], x_words[0].rearrange("p n t -> p (n t)").bitcast(I32))
        for q in range(QUADS):
            eng = nc.sync
            r = 32 * q + W_ROW
            eng.dma_start(ws[r : r + 4, :].bitcast(I32), w1_scales[0, 4 * q : 4 * q + 4, :].bitcast(I32))
        nc.sync.dma_start(gs_t[:], gs.rearrange("(p t) o -> p (t o)", t=PACK))

        def deal(eng, dst, src):
            eng.tensor_copy(
                dst.rearrange("p (t m) -> p t m", t=PACK), src.rearrange("p (m t) -> p t m", t=PACK)
            )

        def deal_words(dst, src):
            nc.vector.tensor_copy(
                dst.rearrange("p (t b i) -> p b t i", t=PACK, i=4), src.rearrange("p (b i t) -> p b t i", t=PACK, i=4)
            )

        wwd = tile("wwd", [P, H], U32)
        wsd = tile("wsd", [P, H], U8)
        deal_words(wwd[:], ww[:].bitcast(U32))

        tok_s = tile("tok_s", [P, S], U8)
        can_s = tile("can_s", [P, V], U8)
        nc.vector.tensor_copy(tok_s[:], xs[:].indirect(offs_t[:]))
        deal(nc.vector, wsd[:], ws[:])
        nc.vector.tensor_copy(can_s[:], xs[:].indirect(cand_t[:]))

        early_w = tile("early_w", [P, HALF], U32)
        late_w = tile("late_w", [P, HALF + V], U32, tag="undealt")
        tok_w = [early_w[:], late_w[:, :HALF]]
        for a in range(2):
            nc.vector.tensor_copy(
                tok_w[a],
                xw[:].bitcast(U32).indirect(offs_t[:, a * HALF // 16 : (a + 1) * HALF // 16]),
            )
        can_wd = late_w[:, HALF:]
        nc.vector.tensor_copy(can_wd.rearrange("p (t m) -> p m t", t=PACK), xw[:].bitcast(U32).indirect(cand_t[:]))

        cols = [slice(c * CHUNK, (c + 1) * CHUNK) for c in range(CHUNKS)]
        hid = []
        for c in range(CHUNKS):
            bank = ps.tile([P, PACK, CHUNK], F32, name=f"pre{c}")
            for t in range(PACK):
                nc.tensor.matmul_mx(
                    out=bank[:, t, :],
                    lhsT=wwd[:, t * P : (t + 1) * P].bitcast(FP8X4),
                    lhsT_scale=wsd[W_ROW:P, t * P : (t + 1) * P],
                    rhs=tok_w[c // 2][:, cols[c % 2]].bitcast(FP8X4),
                    rhs_scale=tok_s[:, cols[c]],
                    start=True,
                    stop=True,
                )
            h = tile(f"h{c}", [P, CHUNK, PACK], F32)
            nc.scalar.activation(h[:], bank[:].rearrange("p t n -> p n t"), ACT.Gelu_apprx_tanh)
            hid.append(h)

        z_w = tile("z_w", [P, S], U32)
        z_s = tile("z_s", [P, S], U8)
        gain = gs_t[:].unsqueeze(1).to_broadcast([P, CHUNK, PACK])
        zb = [tile(f"zb{c}", [P, CHUNK, PACK], BF16) for c in range(CHUNKS)]

        def scale_z(c):
            nc.vector.tensor_tensor(zb[c][:], hid[c][:], gain, MULT)

        def quant_z(c):
            nc.vector.quantize_mx(
                out=z_w[:, cols[c]].bitcast(FP8X4), scales=z_s[:, cols[c]], in_=zb[c][:].rearrange("p n t -> p (n t)")
            )

        scale_z(0)
        can_sd = tile("can_sd", [P, V], U8, tag="h0")
        deal(nc.vector, can_sd[:], can_s[:])
        quant_z(0)
        scale_z(1)
        for c in range(2, CHUNKS):
            scale_z(c)
            quant_z(c - 1)
        quant_z(CHUNKS - 1)

        th = []
        out_rows = out_0.rearrange("(p t) n -> p t n", t=PACK)

        def cap(c, mul):
            y = tile(f"y{c}", [P, PACK, CHUNK], F32)
            mul(y[:], th[c][:], 4.0)
            nc.sync.dma_start(out_rows[:, :, cols[c]], y[:])

        for c in range(CHUNKS):
            bank = ps.tile([P, PACK, CHUNK], F32, name=f"score{c}")
            for t in range(PACK):
                nc.tensor.matmul_mx(
                    out=bank[:, t, :],
                    lhsT=can_wd[:, t * P : (t + 1) * P].bitcast(FP8X4),
                    lhsT_scale=can_sd[:, t * P : (t + 1) * P],
                    rhs=z_w[:, cols[c]].bitcast(FP8X4),
                    rhs_scale=z_s[:, cols[c]],
                    start=True,
                    stop=True,
                )
            tt = tile(f"th{c}", [P, PACK, CHUNK], F32)
            nc.scalar.activation(tt[:], bank[:], ACT.Tanh, scale=0.25 * 0.0625)
            th.append(tt)
            if c in SCALAR_CAP:
                cap(c, nc.scalar.mul)

        o_w = tile("o_w", [P, S], U32)
        o_s = tile("o_s", [P, S], U8)
        words_out = out_1[0].rearrange("p n t -> p (n t)").bitcast(I32)
        for c in range(CHUNKS):
            yb = tile(f"yb{c}", [P, CHUNK, PACK], BF16)
            nc.vector.tensor_scalar_mul(
                yb[:].rearrange("p (b i) t -> p b t i", i=4), th[c][:].rearrange("p t (b i) -> p b t i", i=4), 4.0
            )
            if c not in SCALAR_CAP:
                cap(c, nc.vector.tensor_scalar_mul)
            nc.vector.quantize_mx(
                out=o_w[:, cols[c]].bitcast(FP8X4), scales=o_s[:, cols[c]], in_=yb[:].rearrange("p n t -> p (n t)")
            )
            if c % 2 == 1:
                half = slice((c - 1) * CHUNK, (c + 1) * CHUNK)
                nc.sync.dma_start(words_out[:, half], o_w[:, half].bitcast(I32))
        for q in range(QUADS):
            eng = nc.sync if q == QUADS - 1 else nc.scalar
            eng.dma_start(out_2[0, 4 * q : 4 * q + 4, :].bitcast(I32), o_s[32 * q : 32 * q + 4, :].bitcast(I32))
